import numpy as np
import ml_dtypes


def mxq(x, axis, fmt="e4m3"):
    dtype, down = {"e4m3": (ml_dtypes.float8_e4m3fn, 7), "e5m2": (ml_dtypes.float8_e5m2, 14)}[fmt]
    v = np.moveaxis(np.asarray(x, np.float32).astype(ml_dtypes.bfloat16).astype(np.float64), axis, -1)
    blocks = v.reshape(v.shape[:-1] + (-1, 32))
    amax = np.abs(blocks).max(-1, keepdims=True)
    byte = np.maximum(np.where(amax > 0, np.frexp(amax)[1] - 1 + 127, 0) - down, 1)
    scale = np.exp2(byte - 127.0)
    codes = (blocks / scale).astype(np.float32).astype(dtype).astype(np.float64)
    return np.moveaxis((codes * scale).reshape(v.shape), -1, axis)


WIDE = False


def mx_kscale(k):
    if not WIDE:
        return np.ones(k)
    levels = np.array([10, -10, 5, -5, 0])
    if k % 512:
        return np.exp2(np.random.permutation(np.resize(levels, k // 32))).repeat(32)
    a = np.empty((k // 512, 16))
    for p in range(k // 512):
        a[p, :8] = np.random.permutation(np.resize(levels, 8))
        for g in range(8):
            far = levels[np.abs(levels - a[p, g]) >= 10]
            a[p, g + 8] = far[np.random.randint(len(far))]
    return np.exp2(a.ravel()).repeat(32)


BF16 = ml_dtypes.bfloat16


def bf(x):
    return np.asarray(x, np.float32).astype(BF16)


def f64(x):
    return np.asarray(x).astype(np.float64)


T, D, R = 6144, 512, 512


def silu(v):
    return v * (1.0 / (1.0 + np.exp(-v)))


def draw0():
    s, t = mx_kscale(D), mx_kscale(R)
    return {
        "h": bf(np.random.standard_normal((T, D)) * s),
        "rot_in": bf(np.random.standard_normal((R, D)) / np.sqrt(D) / s[None, :]),
        "w": bf(np.random.standard_normal((D, R)) / np.sqrt(D) / s[:, None]),
        "b": bf(0.3 * np.random.standard_normal(R)),
        "g": bf((1.0 + 0.1 * np.random.standard_normal(R)) * t),
        "rot_out": bf(np.random.standard_normal((R, D)) / np.sqrt(R) / t[:, None]),
        "pw": bf(np.random.uniform(0.3, 1.0, T)),
    }


def core(h, rot_in, w, b, g, rot_out, pw):
    hq = mxq(f64(h), 1, "e4m3")
    base = hq @ mxq(f64(rot_in), 1, "e4m3").T
    pre = (hq @ mxq(f64(w), 0, "e4m3")) + f64(b)[None, :]
    src = silu(pre)
    diff = (src - base) * f64(g)[None, :]
    e = mxq(diff, 1, "e4m3") @ mxq(f64(rot_out), 0, "e4m3")
    return f64(pw)[:, None] * e


def e4m3fn_bytes(y):
    return np.clip(np.asarray(y, np.float64), -448.0, 448.0).astype(np.float32).astype(ml_dtypes.float8_e4m3fn).view(np.uint8)


def e4m3fn_values(b):
    return np.asarray(b, np.uint8).view(ml_dtypes.float8_e4m3fn).astype(np.float64)


def setup_inputs():
    d = draw0()
    x0 = np.asarray(d['h']).astype(np.float64)
    s = (np.max(np.abs(x0), axis=(0,), keepdims=True) / 448.0).astype(np.float32)
    out = {}
    for k, v in d.items():
        if k == 'h':
            out['h_bytes'] = e4m3fn_bytes(x0 / s.astype(np.float64))
            out['h_scale'] = s
        else:
            out[k] = v
    return out


def reference(h_bytes, h_scale, rot_in, w, b, g, rot_out, pw):
    return core(e4m3fn_values(h_bytes) * h_scale.astype(np.float64), rot_in, w, b, g, rot_out, pw)

@@ -1,0 +1,263 @@
+from contextlib import ExitStack
+
+import concourse.mybir as mybir
+from concourse.masks import make_identity
+
+T, D, R = 6144, 512, 512
+FLOPS = 3 * 2 * T * D * R
+
+F32 = mybir.dt.float32
+BF16 = mybir.dt.bfloat16
+U32 = mybir.dt.uint32
+U8 = mybir.dt.uint8
+FP8 = mybir.dt.float8_e4m3fn
+FP8X4 = mybir.dt.float8_e4m3fn_x4
+ALU = mybir.AluOpType
+ACT = mybir.ActivationFunctionType
+
+P = 128
+PACK = 4
+TILES = T // P
+GROUPS = TILES // 4
+HALVES = 2 * GROUPS
+COLS = 4 * P
+HCOLS = 2 * P
+V_CAST = 384
+
+
+def tile_loreftsubspaceintervention_t_kernel(tc, h_bytes, h_scale, rot_in, w, b, g, rot_out, pw, out):
+    nc = tc.nc
+    h_rows = h_bytes.rearrange("(p i) k -> p i k", p=P)
+    out_rows = out.rearrange("(p i) d -> p i d", p=P)
+
+    with ExitStack() as ctx:
+        keep = ctx.enter_context(tc.tile_pool(name="keep", bufs=1))
+        hb_pool = ctx.enter_context(tc.tile_pool(name="hb", bufs=3))
+        hg_pool = ctx.enter_context(tc.tile_pool(name="hg", bufs=3))
+        src_pool = ctx.enter_context(tc.tile_pool(name="src", bufs=4))
+        diff_pool = ctx.enter_context(tc.tile_pool(name="diff", bufs=3))
+        dg_pool = ctx.enter_context(tc.tile_pool(name="dg", bufs=3))
+        o_pool = ctx.enter_context(tc.tile_pool(name="o", bufs=4))
+        xt_psum = ctx.enter_context(tc.psum_pool(name="xt", bufs=2))
+        pre_psum = ctx.enter_context(tc.psum_pool(name="pre", bufs=2))
+        base_psum = ctx.enter_context(tc.psum_pool(name="base", bufs=2))
+        edit_psum = ctx.enter_context(tc.psum_pool(name="edit", bufs=2))
+
+        ident = keep.tile([P, P], F32)
+        h_raw = [keep.tile([P, 4, D], U8, name="h_raw_%d" % i) for i in range(GROUPS)]
+        k_scale = keep.tile([P, PACK], F32)
+        rot_in_raw = keep.tile([P, 4, D], BF16)
+        w_raw = keep.tile([P, PACK, R], BF16)
+        rot_out_raw = keep.tile([P, PACK, D], BF16)
+        bias = keep.tile([P, PACK], BF16)
+        gain = keep.tile([P, PACK], BF16)
+        pw_raw = keep.tile([P, TILES], BF16)
+        strength = keep.tile([P, TILES], F32)
+        warm = keep.tile([P, 1], F32)
+
+        w_grouped = keep.tile([P, R * PACK], BF16, align_bytes=64)
+        rot_in_grouped = keep.tile([P, R * PACK], BF16, align_bytes=64)
+        rot_out_grouped = keep.tile([P, D * PACK], BF16, align_bytes=64)
+        w_codes = keep.tile([P, R], U32, align_bytes=64)
+        w_planes = keep.tile([P, R], U8, align_bytes=64)
+        rot_in_codes = keep.tile([P, R], U32, align_bytes=64)
+        rot_in_planes = keep.tile([P, R], U8, align_bytes=64)
+        rot_out_codes = keep.tile([P, D], U32, align_bytes=64)
+        rot_out_planes = keep.tile([P, D], U8, align_bytes=64)
+
+        with tc.manual_schedule():
+            nc.sync.dma_start(out=h_raw[0][:], in_=h_rows[:, 0:4, :])
+            nc.sync.dma_start(out=k_scale[:], in_=h_scale.rearrange("o (p t) -> p (o t)", t=PACK))
+            nc.sync.dma_start(out=w_raw[:], in_=w.rearrange("(p j) c -> p j c", j=PACK))
+            nc.sync.dma_start(out=rot_in_raw[:], in_=rot_in.rearrange("(m t) k -> m t k", t=4))
+            nc.sync.dma_start(out=h_raw[1][:], in_=h_rows[:, 4:8, :])
+            nc.sync.dma_start(out=bias[:], in_=b.rearrange("(p t) -> p t", t=PACK))
+            nc.sync.dma_start(out=gain[:], in_=g.rearrange("(p t) -> p t", t=PACK))
+            nc.sync.dma_start(out=rot_out_raw[:], in_=rot_out.rearrange("(p j) n -> p j n", j=PACK))
+            nc.sync.dma_start(out=pw_raw[:], in_=pw.rearrange("(p i) -> p i", p=P))
+            for i in range(2, GROUPS):
+                nc.sync.dma_start(out=h_raw[i][:], in_=h_rows[:, 4 * i : 4 * i + 4, :])
+
+            nc.vector.memset(warm[:], 0.0)
+            nc.scalar.activation(out=warm[:], in_=warm[:], func=ACT.Silu)
+            make_identity(nc, ident[:])
+
+            hb, xt, hg, hq, diff, dq, edit_in = {}, {}, {}, {}, {}, {}, {}
+
+            def widen(n):
+                i, half = divmod(n, 2)
+                codes = h_raw[i][:].rearrange("p j k -> p (j k)")
+                tokens = hb_pool.tile([P, 2 * D], BF16)
+                lo = half * 2 * D
+                cut = 2 * D - V_CAST
+                nc.scalar.copy(out=tokens[:, :cut], in_=codes[:, lo : lo + cut].bitcast(FP8))
+                nc.vector.tensor_copy(out=tokens[:, cut:], in_=codes[:, lo + cut : lo + 2 * D].bitcast(FP8))
+                hb[n] = tokens
+
+            def turn(n):
+                bank = xt_psum.tile([P, 2, HCOLS], F32)
+                words = hb.pop(n)[:].bitcast(F32)
+                for j in range(2):
+                    for u in range(2):
+                        nc.tensor.transpose(bank[:, u, j * P : (j + 1) * P], words[:, j * 256 + u : (j + 1) * 256 : 2], ident[:])
+                xt[n] = bank
+
+            def scale_h(n):
+                i, half = divmod(n, 2)
+                if half == 0:
+                    grouped = hg_pool.tile([P, COLS, PACK], BF16, align_bytes=64)
+                    hg[i] = grouped
+                dst = hg[i][:, half * HCOLS : (half + 1) * HCOLS, :].rearrange("p c (u e) -> p c u e", e=2)
+                src = xt.pop(n)[:].rearrange("p u c -> p (u c)").bitcast(BF16).rearrange("p (u c e) -> p c u e", u=2, e=2)
+                fac = k_scale[:].unsqueeze(1).to_broadcast([P, HCOLS, PACK]).rearrange("p c (u e) -> p c u e", e=2)
+                nc.vector.tensor_tensor(out=dst, in0=src, in1=fac, op=ALU.mult)
+
+            def quantize(codes, planes, grouped):
+                nc.vector.quantize_mx(out=codes.bitcast(FP8X4), scales=planes, in_=grouped)
+
+            def quantize_h(i):
+                codes = hg_pool.tile([P, COLS], U32, align_bytes=64, name="h_codes")
+                planes = hg_pool.tile([P, COLS], U8, align_bytes=64, name="h_planes")
+                quantize(codes[:], planes[:], hg.pop(i)[:].rearrange("p c t -> p (c t)"))
+                hq[i] = (codes, planes)
+
+            def quantize_diff(i):
+                codes = dg_pool.tile([P, COLS], U32, align_bytes=64, name="d_codes")
+                planes = dg_pool.tile([P, COLS], U8, align_bytes=64, name="d_planes")
+                quantize(codes[:], planes[:], edit_in.pop(i)[:].rearrange("p c t -> p (c t)"))
+                dq[i] = (codes, planes)
+
+            def project(n):
+                i, half = divmod(n, 2)
+                codes, planes = hq[i]
+                pairs = []
+                for t in (2 * half, 2 * half + 1):
+                    rows = slice(t * P, (t + 1) * P)
+                    pre = pre_psum.tile([P, COLS], F32)
+                    base = base_psum.tile([P, COLS], F32)
+                    for bank, lc, lp in ((pre, w_codes, w_planes), (base, rot_in_codes, rot_in_planes)):
+                        nc.tensor.matmul_mx(
+                            out=bank[:],
+                            lhsT=lc[:, rows].bitcast(FP8X4),
+                            lhsT_scale=lp[:, rows],
+                            rhs=codes[:].bitcast(FP8X4),
+                            rhs_scale=planes[:],
+                            start=True,
+                            stop=True,
+                        )
+                    pairs.append((t, pre, base))
+                return pairs
+
+            def activate(pairs):
+                res = []
+                for t, pre, base in pairs:
+                    src = src_pool.tile([P, COLS], F32)
+                    nc.scalar.activation(out=src[:], in_=pre[:], func=ACT.Silu, bias=bias[:, t : t + 1])
+                    res.append((t, src, base))
+                return res
+
+            def subtract(n, triples):
+                i, half = divmod(n, 2)
+                if half == 0:
+                    delta = diff_pool.tile([P, 4, COLS], F32)
+                    diff[i] = delta
+                for t, src, base in triples:
+                    nc.vector.tensor_tensor(out=diff[i][:, t, :], in0=src[:], in1=base[:], op=ALU.subtract)
+
+            def apply_gain(n):
+                i, half = divmod(n, 2)
+                if half == 0:
+                    gained = dg_pool.tile([P, COLS, PACK], BF16, align_bytes=64)
+                    edit_in[i] = gained
+                for q in range(2):
+                    cols = slice(half * HCOLS + q * P, half * HCOLS + (q + 1) * P)
+                    nc.gpsimd.tensor_tensor(
+                        out=edit_in[i][:, cols, :],
+                        in0=diff[i][:, :, cols].rearrange("p t c -> p c t"),
+                        in1=gain[:].unsqueeze(1).to_broadcast([P, P, PACK]),
+                        op=ALU.mult,
+                    )
+
+            def expand(n):
+                i, half = divmod(n, 2)
+                codes, planes = dq[i]
+                banks = []
+                for j in (2 * half, 2 * half + 1):
+                    cols = slice(j * P, (j + 1) * P)
+                    edit = edit_psum.tile([P, D], F32)
+                    nc.tensor.matmul_mx(
+                        out=edit[:],
+                        lhsT=codes[:, cols].bitcast(FP8X4),
+                        lhsT_scale=planes[:, cols],
+                        rhs=rot_out_codes[:].bitcast(FP8X4),
+                        rhs_scale=rot_out_planes[:],
+                        start=True,
+                        stop=True,
+                    )
+                    banks.append((4 * i + j, edit))
+                return banks
+
+            def store(n, banks):
+                rows = o_pool.tile([P, 2, D], F32)
+                for q, (tile, edit) in enumerate(banks):
+                    nc.scalar.activation(out=rows[:, q, :], in_=edit[:], func=ACT.Copy, scale=strength[:, tile : tile + 1])
+                nc.sync.dma_start(out=out_rows[:, 2 * n : 2 * n + 2, :], in_=rows[:])
+
+            def w_interleave():
+                dst = w_grouped[:].rearrange("p (t m j) -> p t m j", t=4, j=PACK)
+                src = w_raw[:].rearrange("p j (m t) -> p t m j", t=4)
+                nc.gpsimd.tensor_scalar(out=dst[:, 0:2], in0=src[:, 0:2], scalar1=1.0, scalar2=0.0, op0=ALU.mult, op1=ALU.add)
+                nc.scalar.copy(out=dst[:, 2:4], in_=src[:, 2:4])
+
+            def rot_in_turn():
+                for t0 in (0, 2):
+                    bank = edit_psum.tile([P, 2, HCOLS], F32, name="edit")
+                    for s in range(2):
+                        words = rot_in_raw[:, t0 + s, :].bitcast(F32)
+                        for u in range(2):
+                            nc.tensor.transpose(bank[:, u, s * P : (s + 1) * P], words[:, u::2], ident[:])
+                    dst = rot_in_grouped[:, t0 * COLS : (t0 + 2) * COLS].bitcast(F32).rearrange("p (c u) -> p c u", u=2)
+                    nc.scalar.copy(out=dst, in_=bank[:].rearrange("p u c -> p c u"))
+
+            def step(n):
+                if 0 <= n < HALVES:
+                    pairs = activate(project(n))
+                if n % 2 == 1 and 0 <= (n + 1) // 2 < GROUPS:
+                    quantize_h((n + 1) // 2)
+                if n % 2 == 0 and 0 <= (n - 4) // 2 < GROUPS:
+                    quantize_diff((n - 4) // 2)
+                if 0 <= n < HALVES:
+                    subtract(n, pairs)
+                if 0 <= n + 3 < HALVES:
+                    scale_h(n + 3)
+                if 0 <= n - 2 < HALVES:
+                    apply_gain(n - 2)
+                if 0 <= n - 4 < HALVES:
+                    banks = expand(n - 4)
+                if 0 <= n + 4 < HALVES:
+                    turn(n + 4)
+                if 0 <= n + 5 < HALVES:
+                    widen(n + 5)
+                if 0 <= n - 4 < HALVES:
+                    store(n - 4, banks)
+
+            step(-5)
+            step(-4)
+            w_interleave()
+            rot_in_turn()
+            step(-3)
+            step(-2)
+            quantize(w_codes[:], w_planes[:], w_grouped[:])
+            quantize(rot_in_codes[:], rot_in_planes[:], rot_in_grouped[:])
+            step(-1)
+            nc.gpsimd.tensor_scalar(
+                out=rot_out_grouped[:].rearrange("p (n j) -> p n j", j=PACK),
+                in0=rot_out_raw[:].rearrange("p j n -> p n j"),
+                scalar1=1.0, scalar2=0.0, op0=ALU.mult, op1=ALU.add,
+            )
+            nc.vector.tensor_copy(out=strength[:], in_=pw_raw[:])
+            step(0)
+            step(1)
+            quantize(rot_out_codes[:], rot_out_planes[:], rot_out_grouped[:])
+            for n in range(2, HALVES + 4):
+                step(n)

@@ -22,7 +22,8 @@ GROUPS = TILES // 4
 HALVES = 2 * GROUPS
 COLS = 4 * P
 HCOLS = 2 * P
-V_CAST = 384
+LAG = 3
+RUN = 4
 
 
 def tile_loreftsubspaceintervention_t_kernel(tc, h_bytes, h_scale, rot_in, w, b, g, rot_out, pw, out):
@@ -33,10 +34,10 @@ def tile_loreftsubspaceintervention_t_kernel(tc, h_bytes, h_scale, rot_in, w, b,
     with ExitStack() as ctx:
         keep = ctx.enter_context(tc.tile_pool(name="keep", bufs=1))
         hb_pool = ctx.enter_context(tc.tile_pool(name="hb", bufs=3))
-        hg_pool = ctx.enter_context(tc.tile_pool(name="hg", bufs=3))
+        hg_pool = ctx.enter_context(tc.tile_pool(name="hg", bufs=4))
         src_pool = ctx.enter_context(tc.tile_pool(name="src", bufs=4))
         diff_pool = ctx.enter_context(tc.tile_pool(name="diff", bufs=3))
-        dg_pool = ctx.enter_context(tc.tile_pool(name="dg", bufs=3))
+        hq_pool = ctx.enter_context(tc.tile_pool(name="hq", bufs=5))
         o_pool = ctx.enter_context(tc.tile_pool(name="o", bufs=4))
         xt_psum = ctx.enter_context(tc.psum_pool(name="xt", bufs=2))
         pre_psum = ctx.enter_context(tc.psum_pool(name="pre", bufs=2))
@@ -82,16 +83,14 @@ def tile_loreftsubspaceintervention_t_kernel(tc, h_bytes, h_scale, rot_in, w, b,
             nc.scalar.activation(out=warm[:], in_=warm[:], func=ACT.Silu)
             make_identity(nc, ident[:])
 
-            hb, xt, hg, hq, diff, dq, edit_in = {}, {}, {}, {}, {}, {}, {}
+            hb, xt, joint, hq, diff, dq = {}, {}, {}, {}, {}, {}
 
             def widen(n):
                 i, half = divmod(n, 2)
                 codes = h_raw[i][:].rearrange("p j k -> p (j k)")
                 tokens = hb_pool.tile([P, 2 * D], BF16)
                 lo = half * 2 * D
-                cut = 2 * D - V_CAST
-                nc.scalar.copy(out=tokens[:, :cut], in_=codes[:, lo : lo + cut].bitcast(FP8))
-                nc.vector.tensor_copy(out=tokens[:, cut:], in_=codes[:, lo + cut : lo + 2 * D].bitcast(FP8))
+                nc.scalar.copy(out=tokens[:], in_=codes[:, lo : lo + 2 * D].bitcast(FP8))
                 hb[n] = tokens
 
             def turn(n):
@@ -102,12 +101,17 @@ def tile_loreftsubspaceintervention_t_kernel(tc, h_bytes, h_scale, rot_in, w, b,
                         nc.tensor.transpose(bank[:, u, j * P : (j + 1) * P], words[:, j * 256 + u : (j + 1) * 256 : 2], ident[:])
                 xt[n] = bank
 
+            def get_joint(i):
+                if i not in joint:
+                    both = hg_pool.tile([P, 2 * COLS, PACK], BF16, align_bytes=64)
+                    joint[i] = both
+                return joint[i]
+
             def scale_h(n):
                 i, half = divmod(n, 2)
                 if half == 0:
-                    grouped = hg_pool.tile([P, COLS, PACK], BF16, align_bytes=64)
-                    hg[i] = grouped
-                dst = hg[i][:, half * HCOLS : (half + 1) * HCOLS, :].rearrange("p c (u e) -> p c u e", e=2)
+                    get_joint(i)
+                dst = joint[i][:, half * HCOLS : (half + 1) * HCOLS, :].rearrange("p c (u e) -> p c u e", e=2)
                 src = xt.pop(n)[:].rearrange("p u c -> p (u c)").bitcast(BF16).rearrange("p (u c e) -> p c u e", u=2, e=2)
                 fac = k_scale[:].unsqueeze(1).to_broadcast([P, HCOLS, PACK]).rearrange("p c (u e) -> p c u e", e=2)
                 nc.vector.tensor_tensor(out=dst, in0=src, in1=fac, op=ALU.mult)
@@ -115,17 +119,17 @@ def tile_loreftsubspaceintervention_t_kernel(tc, h_bytes, h_scale, rot_in, w, b,
             def quantize(codes, planes, grouped):
                 nc.vector.quantize_mx(out=codes.bitcast(FP8X4), scales=planes, in_=grouped)
 
-            def quantize_h(i):
-                codes = hg_pool.tile([P, COLS], U32, align_bytes=64, name="h_codes")
-                planes = hg_pool.tile([P, COLS], U8, align_bytes=64, name="h_planes")
-                quantize(codes[:], planes[:], hg.pop(i)[:].rearrange("p c t -> p (c t)"))
-                hq[i] = (codes, planes)
-
-            def quantize_diff(i):
-                codes = dg_pool.tile([P, COLS], U32, align_bytes=64, name="d_codes")
-                planes = dg_pool.tile([P, COLS], U8, align_bytes=64, name="d_planes")
-                quantize(codes[:], planes[:], edit_in.pop(i)[:].rearrange("p c t -> p (c t)"))
-                dq[i] = (codes, planes)
+            def quantize_joint(i):
+                first = 0 if i < GROUPS else COLS
+                last = 2 * COLS if i >= LAG else COLS
+                codes = hq_pool.tile([P, 2 * COLS], U32, align_bytes=64)
+                planes = hq_pool.tile([P, 2 * COLS], U8, align_bytes=64)
+                grouped = joint.pop(i)[:, first:last, :].rearrange("p c t -> p (c t)")
+                quantize(codes[:, first:last], planes[:, first:last], grouped)
+                if i < GROUPS:
+                    hq[i] = (codes[:, :COLS], planes[:, :COLS])
+                if i >= LAG:
+                    dq[i - LAG] = (codes[:, COLS:], planes[:, COLS:])
 
             def project(n):
                 i, half = divmod(n, 2)
@@ -140,8 +144,8 @@ def tile_loreftsubspaceintervention_t_kernel(tc, h_bytes, h_scale, rot_in, w, b,
                             out=bank[:],
                             lhsT=lc[:, rows].bitcast(FP8X4),
                             lhsT_scale=lp[:, rows],
-                            rhs=codes[:].bitcast(FP8X4),
-                            rhs_scale=planes[:],
+                            rhs=codes.bitcast(FP8X4),
+                            rhs_scale=planes,
                             start=True,
                             stop=True,
                         )
@@ -166,15 +170,13 @@ def tile_loreftsubspaceintervention_t_kernel(tc, h_bytes, h_scale, rot_in, w, b,
 
             def apply_gain(n):
                 i, half = divmod(n, 2)
-                if half == 0:
-                    gained = dg_pool.tile([P, COLS, PACK], BF16, align_bytes=64)
-                    edit_in[i] = gained
+                gained = get_joint(i + LAG)
                 for q in range(2):
-                    cols = slice(half * HCOLS + q * P, half * HCOLS + (q + 1) * P)
+                    lo = half * HCOLS + q * P
                     nc.gpsimd.tensor_tensor(
-                        out=edit_in[i][:, cols, :],
-                        in0=diff[i][:, :, cols].rearrange("p t c -> p c t"),
-                        in1=gain[:].unsqueeze(1).to_broadcast([P, P, PACK]),
+                        out=gained[:, COLS + lo : COLS + lo + P, :].rearrange("p (c i) t -> p c t i", i=RUN),
+                        in0=diff[i][:, :, lo : lo + P].rearrange("p t (c i) -> p c t i", i=RUN),
+                        in1=gain[:].unsqueeze(1).unsqueeze(3).to_broadcast([P, P // RUN, PACK, RUN]),
                         op=ALU.mult,
                     )
 
@@ -200,7 +202,10 @@ def tile_loreftsubspaceintervention_t_kernel(tc, h_bytes, h_scale, rot_in, w, b,
             def store(n, banks):
                 rows = o_pool.tile([P, 2, D], F32)
                 for q, (tile, edit) in enumerate(banks):
-                    nc.scalar.activation(out=rows[:, q, :], in_=edit[:], func=ACT.Copy, scale=strength[:, tile : tile + 1])
+                    if tile % 4 == 3:
+                        nc.vector.tensor_scalar(out=rows[:, q, :], in0=edit[:], scalar1=strength[:, tile : tile + 1], scalar2=None, op0=ALU.mult)
+                    else:
+                        nc.scalar.activation(out=rows[:, q, :], in_=edit[:], func=ACT.Copy, scale=strength[:, tile : tile + 1])
                 nc.sync.dma_start(out=out_rows[:, 2 * n : 2 * n + 2, :], in_=rows[:])
 
             def w_interleave():
@@ -222,24 +227,22 @@ def tile_loreftsubspaceintervention_t_kernel(tc, h_bytes, h_scale, rot_in, w, b,
             def step(n):
                 if 0 <= n < HALVES:
                     pairs = activate(project(n))
-                if n % 2 == 1 and 0 <= (n + 1) // 2 < GROUPS:
-                    quantize_h((n + 1) // 2)
-                if n % 2 == 0 and 0 <= (n - 4) // 2 < GROUPS:
-                    quantize_diff((n - 4) // 2)
+                if n % 2 == 1 and 0 <= (n + 1) // 2 < GROUPS + LAG:
+                    quantize_joint((n + 1) // 2)
                 if 0 <= n < HALVES:
                     subtract(n, pairs)
                 if 0 <= n + 3 < HALVES:
                     scale_h(n + 3)
                 if 0 <= n - 2 < HALVES:
                     apply_gain(n - 2)
-                if 0 <= n - 4 < HALVES:
-                    banks = expand(n - 4)
+                if 0 <= n - 6 < HALVES:
+                    banks = expand(n - 6)
                 if 0 <= n + 4 < HALVES:
                     turn(n + 4)
                 if 0 <= n + 5 < HALVES:
                     widen(n + 5)
-                if 0 <= n - 4 < HALVES:
-                    store(n - 4, banks)
+                if 0 <= n - 6 < HALVES:
+                    store(n - 6, banks)
 
             step(-5)
             step(-4)
@@ -259,5 +262,5 @@ def tile_loreftsubspaceintervention_t_kernel(tc, h_bytes, h_scale, rot_in, w, b,
             step(0)
             step(1)
             quantize(rot_out_codes[:], rot_out_planes[:], rot_out_grouped[:])
-            for n in range(2, HALVES + 4):
+            for n in range(2, HALVES + 6):
                 step(n)

@@ -35,8 +35,8 @@ def tile_loreftsubspaceintervention_t_kernel(tc, h_bytes, h_scale, rot_in, w, b,
         keep = ctx.enter_context(tc.tile_pool(name="keep", bufs=1))
         hb_pool = ctx.enter_context(tc.tile_pool(name="hb", bufs=3))
         hg_pool = ctx.enter_context(tc.tile_pool(name="hg", bufs=4))
-        src_pool = ctx.enter_context(tc.tile_pool(name="src", bufs=4))
-        diff_pool = ctx.enter_context(tc.tile_pool(name="diff", bufs=3))
+        src_pool = ctx.enter_context(tc.tile_pool(name="src", bufs=3))
+        diff_pool = ctx.enter_context(tc.tile_pool(name="diff", bufs=8))
         hq_pool = ctx.enter_context(tc.tile_pool(name="hq", bufs=5))
         o_pool = ctx.enter_context(tc.tile_pool(name="o", bufs=4))
         xt_psum = ctx.enter_context(tc.psum_pool(name="xt", bufs=2))
@@ -52,6 +52,7 @@ def tile_loreftsubspaceintervention_t_kernel(tc, h_bytes, h_scale, rot_in, w, b,
         rot_out_raw = keep.tile([P, PACK, D], BF16)
         bias = keep.tile([P, PACK], BF16)
         gain = keep.tile([P, PACK], BF16)
+        gain_rows = keep.tile([P, P, PACK], F32)
         pw_raw = keep.tile([P, TILES], BF16)
         strength = keep.tile([P, TILES], F32)
         warm = keep.tile([P, 1], F32)
@@ -59,19 +60,16 @@ def tile_loreftsubspaceintervention_t_kernel(tc, h_bytes, h_scale, rot_in, w, b,
         w_grouped = keep.tile([P, R * PACK], BF16, align_bytes=64)
         rot_in_grouped = keep.tile([P, R * PACK], BF16, align_bytes=64)
         rot_out_grouped = keep.tile([P, D * PACK], BF16, align_bytes=64)
-        w_codes = keep.tile([P, R], U32, align_bytes=64)
-        w_planes = keep.tile([P, R], U8, align_bytes=64)
-        rot_in_codes = keep.tile([P, R], U32, align_bytes=64)
-        rot_in_planes = keep.tile([P, R], U8, align_bytes=64)
-        rot_out_codes = keep.tile([P, D], U32, align_bytes=64)
-        rot_out_planes = keep.tile([P, D], U8, align_bytes=64)
+        w_q = (keep.tile([P, R], U32, align_bytes=64, name="w_codes"), keep.tile([P, R], U8, align_bytes=64, name="w_planes"))
+        rot_in_q = (keep.tile([P, R], U32, align_bytes=64, name="rot_in_codes"), keep.tile([P, R], U8, align_bytes=64, name="rot_in_planes"))
+        rot_out_q = (keep.tile([P, D], U32, align_bytes=64, name="rot_out_codes"), keep.tile([P, D], U8, align_bytes=64, name="rot_out_planes"))
 
         with tc.manual_schedule():
             nc.sync.dma_start(out=h_raw[0][:], in_=h_rows[:, 0:4, :])
             nc.sync.dma_start(out=k_scale[:], in_=h_scale.rearrange("o (p t) -> p (o t)", t=PACK))
             nc.sync.dma_start(out=w_raw[:], in_=w.rearrange("(p j) c -> p j c", j=PACK))
-            nc.sync.dma_start(out=rot_in_raw[:], in_=rot_in.rearrange("(m t) k -> m t k", t=4))
             nc.sync.dma_start(out=h_raw[1][:], in_=h_rows[:, 4:8, :])
+            nc.sync.dma_start(out=rot_in_raw[:], in_=rot_in.rearrange("(m t) k -> m t k", t=4))
             nc.sync.dma_start(out=bias[:], in_=b.rearrange("(p t) -> p t", t=PACK))
             nc.sync.dma_start(out=gain[:], in_=g.rearrange("(p t) -> p t", t=PACK))
             nc.sync.dma_start(out=rot_out_raw[:], in_=rot_out.rearrange("(p j) n -> p j n", j=PACK))
@@ -83,14 +81,15 @@ def tile_loreftsubspaceintervention_t_kernel(tc, h_bytes, h_scale, rot_in, w, b,
             nc.scalar.activation(out=warm[:], in_=warm[:], func=ACT.Silu)
             make_identity(nc, ident[:])
 
-            hb, xt, joint, hq, diff, dq = {}, {}, {}, {}, {}, {}
+            pres, bases, edits = [], [], []
+            hb, xt, joint, hq, src, diff, dq = {}, {}, {}, {}, {}, {}, {}
 
-            def widen(n):
+            def widen(n, copy):
                 i, half = divmod(n, 2)
                 codes = h_raw[i][:].rearrange("p j k -> p (j k)")
                 tokens = hb_pool.tile([P, 2 * D], BF16)
                 lo = half * 2 * D
-                nc.scalar.copy(out=tokens[:], in_=codes[:, lo : lo + 2 * D].bitcast(FP8))
+                copy(out=tokens[:], in_=codes[:, lo : lo + 2 * D].bitcast(FP8))
                 hb[n] = tokens
 
             def turn(n):
@@ -122,97 +121,100 @@ def tile_loreftsubspaceintervention_t_kernel(tc, h_bytes, h_scale, rot_in, w, b,
             def quantize_joint(i):
                 first = 0 if i < GROUPS else COLS
                 last = 2 * COLS if i >= LAG else COLS
+                parts = 2 if i == GROUPS + LAG - 1 else 1
+                width = (last - first) // parts
                 codes = hq_pool.tile([P, 2 * COLS], U32, align_bytes=64)
                 planes = hq_pool.tile([P, 2 * COLS], U8, align_bytes=64)
-                grouped = joint.pop(i)[:, first:last, :].rearrange("p c t -> p (c t)")
-                quantize(codes[:, first:last], planes[:, first:last], grouped)
+                grouped = joint.pop(i)
+                for lo in range(first, last, width):
+                    cols = slice(lo, lo + width)
+                    quantize(codes[:, cols], planes[:, cols], grouped[:, cols, :].rearrange("p c t -> p (c t)"))
                 if i < GROUPS:
                     hq[i] = (codes[:, :COLS], planes[:, :COLS])
                 if i >= LAG:
                     dq[i - LAG] = (codes[:, COLS:], planes[:, COLS:])
 
-            def project(n):
-                i, half = divmod(n, 2)
-                codes, planes = hq[i]
-                pairs = []
-                for t in (2 * half, 2 * half + 1):
-                    rows = slice(t * P, (t + 1) * P)
-                    pre = pre_psum.tile([P, COLS], F32)
-                    base = base_psum.tile([P, COLS], F32)
-                    for bank, lc, lp in ((pre, w_codes, w_planes), (base, rot_in_codes, rot_in_planes)):
-                        nc.tensor.matmul_mx(
-                            out=bank[:],
-                            lhsT=lc[:, rows].bitcast(FP8X4),
-                            lhsT_scale=lp[:, rows],
-                            rhs=codes.bitcast(FP8X4),
-                            rhs_scale=planes,
-                            start=True,
-                            stop=True,
-                        )
-                    pairs.append((t, pre, base))
-                return pairs
+            def multiply(bank, left, left_cols, right, right_cols):
+                nc.tensor.matmul_mx(
+                    out=bank,
+                    lhsT=left[0][:, left_cols].bitcast(FP8X4),
+                    lhsT_scale=left[1][:, left_cols],
+                    rhs=right[0][:, right_cols].bitcast(FP8X4),
+                    rhs_scale=right[1][:, right_cols],
+                    start=True,
+                    stop=True,
+                )
 
-            def activate(pairs):
-                res = []
-                for t, pre, base in pairs:
-                    src = src_pool.tile([P, COLS], F32)
-                    nc.scalar.activation(out=src[:], in_=pre[:], func=ACT.Silu, bias=bias[:, t : t + 1])
-                    res.append((t, src, base))
-                return res
-
-            def subtract(n, triples):
+            def project_source(n):
                 i, half = divmod(n, 2)
                 if half == 0:
-                    delta = diff_pool.tile([P, 4, COLS], F32)
-                    diff[i] = delta
-                for t, src, base in triples:
-                    nc.vector.tensor_tensor(out=diff[i][:, t, :], in0=src[:], in1=base[:], op=ALU.subtract)
+                    source = src_pool.tile([P, 4, COLS], F32)
+                    src[i] = source
+                for t in (2 * half, 2 * half + 1):
+                    pre = pre_psum.tile([P, COLS], F32)
+                    multiply(pre[:], w_q, slice(t * P, (t + 1) * P), hq[i], slice(0, COLS))
+                    pres.append((i, t, pre))
+
+            def activate():
+                while pres:
+                    i, t, pre = pres.pop(0)
+                    nc.scalar.activation(out=src[i][:, t, :], in_=pre[:], func=ACT.Silu, bias=bias[:, t : t + 1])
+
+            def project_base(n):
+                i, half = divmod(n, 2)
+                for j in (2 * half, 2 * half + 1):
+                    base = base_psum.tile([P, 4, P], F32)
+                    for t in range(4):
+                        multiply(base[:, t, :], rot_in_q, slice(t * P, (t + 1) * P), hq[i], slice(j * P, (j + 1) * P))
+                    bases.append((i, j, base))
+
+            def subtract():
+                while bases:
+                    i, j, base = bases.pop(0)
+                    cols = slice(j * P, (j + 1) * P)
+                    delta = diff_pool.tile([P, P, PACK], F32)
+                    diff[4 * i + j] = delta
+                    nc.vector.tensor_tensor(
+                        out=delta[:].rearrange("p (c i) t -> p c t i", i=RUN),
+                        in0=src[i][:, :, cols].rearrange("p t (c i) -> p c t i", i=RUN),
+                        in1=base[:].rearrange("p t (c i) -> p c t i", i=RUN),
+                        op=ALU.subtract,
+                    )
 
             def apply_gain(n):
-                i, half = divmod(n, 2)
-                gained = get_joint(i + LAG)
-                for q in range(2):
-                    lo = half * HCOLS + q * P
-                    nc.gpsimd.tensor_tensor(
-                        out=gained[:, COLS + lo : COLS + lo + P, :].rearrange("p (c i) t -> p c t i", i=RUN),
-                        in0=diff[i][:, :, lo : lo + P].rearrange("p t (c i) -> p c t i", i=RUN),
-                        in1=gain[:].unsqueeze(1).unsqueeze(3).to_broadcast([P, P // RUN, PACK, RUN]),
+                for tile in (2 * n, 2 * n + 1):
+                    i, j = divmod(tile, 4)
+                    engine = nc.vector if tile >= TILES - 2 else nc.gpsimd
+                    lo = COLS + j * P
+                    engine.tensor_tensor(
+                        out=get_joint(i + LAG)[:, lo : lo + P, :].rearrange("p c t -> p (c t)"),
+                        in0=diff.pop(tile)[:].rearrange("p c t -> p (c t)"),
+                        in1=gain_rows[:].rearrange("p c t -> p (c t)"),
                         op=ALU.mult,
                     )
 
             def expand(n):
                 i, half = divmod(n, 2)
-                codes, planes = dq[i]
-                banks = []
                 for j in (2 * half, 2 * half + 1):
-                    cols = slice(j * P, (j + 1) * P)
                     edit = edit_psum.tile([P, D], F32)
-                    nc.tensor.matmul_mx(
-                        out=edit[:],
-                        lhsT=codes[:, cols].bitcast(FP8X4),
-                        lhsT_scale=planes[:, cols],
-                        rhs=rot_out_codes[:].bitcast(FP8X4),
-                        rhs_scale=rot_out_planes[:],
-                        start=True,
-                        stop=True,
-                    )
-                    banks.append((4 * i + j, edit))
-                return banks
+                    multiply(edit[:], dq[i], slice(j * P, (j + 1) * P), rot_out_q, slice(0, D))
+                    edits.append((4 * i + j, edit))
 
-            def store(n, banks):
+            def store(n):
                 rows = o_pool.tile([P, 2, D], F32)
-                for q, (tile, edit) in enumerate(banks):
+                for q, (tile, edit) in enumerate(edits):
                     if tile % 4 == 3:
                         nc.vector.tensor_scalar(out=rows[:, q, :], in0=edit[:], scalar1=strength[:, tile : tile + 1], scalar2=None, op0=ALU.mult)
                     else:
                         nc.scalar.activation(out=rows[:, q, :], in_=edit[:], func=ACT.Copy, scale=strength[:, tile : tile + 1])
                 nc.sync.dma_start(out=out_rows[:, 2 * n : 2 * n + 2, :], in_=rows[:])
+                edits.clear()
 
             def w_interleave():
                 dst = w_grouped[:].rearrange("p (t m j) -> p t m j", t=4, j=PACK)
                 src = w_raw[:].rearrange("p j (m t) -> p t m j", t=4)
                 nc.gpsimd.tensor_scalar(out=dst[:, 0:2], in0=src[:, 0:2], scalar1=1.0, scalar2=0.0, op0=ALU.mult, op1=ALU.add)
-                nc.scalar.copy(out=dst[:, 2:4], in_=src[:, 2:4])
+                nc.vector.tensor_copy(out=dst[:, 2:4], in_=src[:, 2:4])
 
             def rot_in_turn():
                 for t0 in (0, 2):
@@ -225,42 +227,54 @@ def tile_loreftsubspaceintervention_t_kernel(tc, h_bytes, h_scale, rot_in, w, b,
                     nc.scalar.copy(out=dst, in_=bank[:].rearrange("p u c -> p c u"))
 
             def step(n):
-                if 0 <= n < HALVES:
-                    pairs = activate(project(n))
+                activate()
+                subtract()
+                if 0 <= n - 7 < HALVES:
+                    store(n - 7)
+                if 0 <= n - 3 < HALVES:
+                    apply_gain(n - 3)
                 if n % 2 == 1 and 0 <= (n + 1) // 2 < GROUPS + LAG:
                     quantize_joint((n + 1) // 2)
-                if 0 <= n < HALVES:
-                    subtract(n, pairs)
                 if 0 <= n + 3 < HALVES:
                     scale_h(n + 3)
-                if 0 <= n - 2 < HALVES:
-                    apply_gain(n - 2)
-                if 0 <= n - 6 < HALVES:
-                    banks = expand(n - 6)
+                if 0 <= n + 5 < HALVES:
+                    widen(n + 5, nc.scalar.copy)
                 if 0 <= n + 4 < HALVES:
                     turn(n + 4)
-                if 0 <= n + 5 < HALVES:
-                    widen(n + 5)
+                if 0 <= n - 2 < HALVES:
+                    project_base(n - 2)
+                if 0 <= n < HALVES:
+                    project_source(n)
                 if 0 <= n - 6 < HALVES:
-                    store(n - 6, banks)
+                    expand(n - 6)
 
-            step(-5)
-            step(-4)
+            widen(0, nc.scalar.copy)
+            widen(1, nc.vector.tensor_copy)
+            turn(0)
             w_interleave()
+            turn(1)
+            scale_h(0)
+            scale_h(1)
+            quantize(w_q[0][:], w_q[1][:], w_grouped[:])
+            quantize_joint(0)
+            widen(2, nc.scalar.copy)
+            widen(3, nc.scalar.copy)
+            turn(2)
+            turn(3)
             rot_in_turn()
-            step(-3)
-            step(-2)
-            quantize(w_codes[:], w_planes[:], w_grouped[:])
-            quantize(rot_in_codes[:], rot_in_planes[:], rot_in_grouped[:])
-            step(-1)
+            scale_h(2)
+            widen(4, nc.scalar.copy)
+            step(0)
+            quantize(rot_in_q[0][:], rot_in_q[1][:], rot_in_grouped[:])
+            nc.vector.tensor_copy(out=gain_rows[:], in_=gain[:].unsqueeze(1).to_broadcast([P, P, PACK]))
+            nc.vector.tensor_copy(out=strength[:], in_=pw_raw[:])
             nc.gpsimd.tensor_scalar(
                 out=rot_out_grouped[:].rearrange("p (n j) -> p n j", j=PACK),
                 in0=rot_out_raw[:].rearrange("p j n -> p n j"),
                 scalar1=1.0, scalar2=0.0, op0=ALU.mult, op1=ALU.add,
             )
-            nc.vector.tensor_copy(out=strength[:], in_=pw_raw[:])
-            step(0)
             step(1)
-            quantize(rot_out_codes[:], rot_out_planes[:], rot_out_grouped[:])
-            for n in range(2, HALVES + 6):
+            step(2)
+            quantize(rot_out_q[0][:], rot_out_q[1][:], rot_out_grouped[:])
+            for n in range(3, HALVES + 7):
                 step(n)

@@ -81,7 +81,7 @@ def tile_loreftsubspaceintervention_t_kernel(tc, h_bytes, h_scale, rot_in, w, b,
             nc.scalar.activation(out=warm[:], in_=warm[:], func=ACT.Silu)
             make_identity(nc, ident[:])
 
-            pres, bases, edits = [], [], []
+            pres, bases, edits, results = [], [], [], {}
             hb, xt, joint, hq, src, diff, dq = {}, {}, {}, {}, {}, {}, {}
 
             def widen(n, copy):
@@ -111,9 +111,9 @@ def tile_loreftsubspaceintervention_t_kernel(tc, h_bytes, h_scale, rot_in, w, b,
                 if half == 0:
                     get_joint(i)
                 dst = joint[i][:, half * HCOLS : (half + 1) * HCOLS, :].rearrange("p c (u e) -> p c u e", e=2)
-                src = xt.pop(n)[:].rearrange("p u c -> p (u c)").bitcast(BF16).rearrange("p (u c e) -> p c u e", u=2, e=2)
+                words = xt.pop(n)[:].rearrange("p u c -> p (u c)").bitcast(BF16).rearrange("p (u c e) -> p c u e", u=2, e=2)
                 fac = k_scale[:].unsqueeze(1).to_broadcast([P, HCOLS, PACK]).rearrange("p c (u e) -> p c u e", e=2)
-                nc.vector.tensor_tensor(out=dst, in0=src, in1=fac, op=ALU.mult)
+                nc.vector.tensor_tensor(out=dst, in0=fac, in1=words, op=ALU.mult)
 
             def quantize(codes, planes, grouped):
                 nc.vector.quantize_mx(out=codes.bitcast(FP8X4), scales=planes, in_=grouped)
@@ -145,28 +145,23 @@ def tile_loreftsubspaceintervention_t_kernel(tc, h_bytes, h_scale, rot_in, w, b,
                     stop=True,
                 )
 
-            def project_source(n):
-                i, half = divmod(n, 2)
-                if half == 0:
+            def project_source(i, t):
+                if t == 0:
                     source = src_pool.tile([P, 4, COLS], F32)
                     src[i] = source
-                for t in (2 * half, 2 * half + 1):
-                    pre = pre_psum.tile([P, COLS], F32)
-                    multiply(pre[:], w_q, slice(t * P, (t + 1) * P), hq[i], slice(0, COLS))
-                    pres.append((i, t, pre))
+                pre = pre_psum.tile([P, COLS], F32)
+                multiply(pre[:], w_q, slice(t * P, (t + 1) * P), hq[i], slice(0, COLS))
+                pres.append((i, t, pre))
 
             def activate():
-                while pres:
-                    i, t, pre = pres.pop(0)
-                    nc.scalar.activation(out=src[i][:, t, :], in_=pre[:], func=ACT.Silu, bias=bias[:, t : t + 1])
+                i, t, pre = pres.pop(0)
+                nc.scalar.activation(out=src[i][:, t, :], in_=pre[:], func=ACT.Silu, bias=bias[:, t : t + 1])
 
-            def project_base(n):
-                i, half = divmod(n, 2)
-                for j in (2 * half, 2 * half + 1):
-                    base = base_psum.tile([P, 4, P], F32)
-                    for t in range(4):
-                        multiply(base[:, t, :], rot_in_q, slice(t * P, (t + 1) * P), hq[i], slice(j * P, (j + 1) * P))
-                    bases.append((i, j, base))
+            def project_base(i, j):
+                base = base_psum.tile([P, 4, P], F32)
+                for t in range(4):
+                    multiply(base[:, t, :], rot_in_q, slice(t * P, (t + 1) * P), hq[i], slice(j * P, (j + 1) * P))
+                bases.append((i, j, base))
 
             def subtract():
                 while bases:
@@ -193,22 +188,23 @@ def tile_loreftsubspaceintervention_t_kernel(tc, h_bytes, h_scale, rot_in, w, b,
                         op=ALU.mult,
                     )
 
-            def expand(n):
-                i, half = divmod(n, 2)
-                for j in (2 * half, 2 * half + 1):
-                    edit = edit_psum.tile([P, D], F32)
-                    multiply(edit[:], dq[i], slice(j * P, (j + 1) * P), rot_out_q, slice(0, D))
-                    edits.append((4 * i + j, edit))
+            def expand(i, j):
+                edit = edit_psum.tile([P, D], F32)
+                multiply(edit[:], dq[i], slice(j * P, (j + 1) * P), rot_out_q, slice(0, D))
+                edits.append((4 * i + j, edit))
 
-            def store(n):
-                rows = o_pool.tile([P, 2, D], F32)
-                for q, (tile, edit) in enumerate(edits):
-                    if tile % 4 == 3:
-                        nc.vector.tensor_scalar(out=rows[:, q, :], in0=edit[:], scalar1=strength[:, tile : tile + 1], scalar2=None, op0=ALU.mult)
-                    else:
-                        nc.scalar.activation(out=rows[:, q, :], in_=edit[:], func=ACT.Copy, scale=strength[:, tile : tile + 1])
-                nc.sync.dma_start(out=out_rows[:, 2 * n : 2 * n + 2, :], in_=rows[:])
-                edits.clear()
+            def finish():
+                tile, edit = edits.pop(0)
+                if tile % 2 == 0:
+                    rows = o_pool.tile([P, 2, D], F32)
+                    results[tile // 2] = rows
+                row = results[tile // 2][:, tile % 2, :]
+                if tile % 6 == 5:
+                    nc.vector.tensor_scalar(out=row, in0=edit[:], scalar1=strength[:, tile : tile + 1], scalar2=None, op0=ALU.mult)
+                else:
+                    nc.scalar.activation(out=row, in_=edit[:], func=ACT.Copy, scale=strength[:, tile : tile + 1])
+                if tile % 2 == 1:
+                    nc.sync.dma_start(out=out_rows[:, tile - 1 : tile + 1, :], in_=results.pop(tile // 2)[:])
 
             def w_interleave():
                 dst = w_grouped[:].rearrange("p (t m j) -> p t m j", t=4, j=PACK)
@@ -226,11 +222,21 @@ def tile_loreftsubspaceintervention_t_kernel(tc, h_bytes, h_scale, rot_in, w, b,
                     dst = rot_in_grouped[:, t0 * COLS : (t0 + 2) * COLS].bitcast(F32).rearrange("p (c u) -> p c u", u=2)
                     nc.scalar.copy(out=dst, in_=bank[:].rearrange("p u c -> p c u"))
 
+            def multiplies(n, k):
+                if 0 <= n - 2 < HALVES:
+                    project_base((n - 2) // 2, 2 * (n % 2) + k)
+                if 0 <= n < HALVES:
+                    project_source(n // 2, 2 * (n % 2) + k)
+                if 0 <= n - 6 < HALVES:
+                    expand((n - 6) // 2, 2 * (n % 2) + k)
+
             def step(n):
-                activate()
                 subtract()
-                if 0 <= n - 7 < HALVES:
-                    store(n - 7)
+                for k in range(2):
+                    if pres:
+                        activate()
+                    if edits:
+                        finish()
                 if 0 <= n - 3 < HALVES:
                     apply_gain(n - 3)
                 if n % 2 == 1 and 0 <= (n + 1) // 2 < GROUPS + LAG:
@@ -239,14 +245,10 @@ def tile_loreftsubspaceintervention_t_kernel(tc, h_bytes, h_scale, rot_in, w, b,
                     scale_h(n + 3)
                 if 0 <= n + 5 < HALVES:
                     widen(n + 5, nc.scalar.copy)
+                multiplies(n, 0)
                 if 0 <= n + 4 < HALVES:
                     turn(n + 4)
-                if 0 <= n - 2 < HALVES:
-                    project_base(n - 2)
-                if 0 <= n < HALVES:
-                    project_source(n)
-                if 0 <= n - 6 < HALVES:
-                    expand(n - 6)
+                multiplies(n, 1)
 
             widen(0, nc.scalar.copy)
             widen(1, nc.vector.tensor_copy)

@@ -12,18 +12,41 @@ U32 = mybir.dt.uint32
 U8 = mybir.dt.uint8
 FP8 = mybir.dt.float8_e4m3fn
 FP8X4 = mybir.dt.float8_e4m3fn_x4
-ALU = mybir.AluOpType
-ACT = mybir.ActivationFunctionType
+MULT = mybir.AluOpType.mult
+ADD = mybir.AluOpType.add
+SUBTRACT = mybir.AluOpType.subtract
+COPY = mybir.ActivationFunctionType.Copy
+SILU = mybir.ActivationFunctionType.Silu
 
 P = 128
 PACK = 4
 TILES = T // P
-GROUPS = TILES // 4
+TILES_PER_GROUP = 4
+GROUPS = TILES // TILES_PER_GROUP
 HALVES = 2 * GROUPS
-COLS = 4 * P
-HCOLS = 2 * P
-LAG = 3
+COLS = TILES_PER_GROUP * P
+HALF_COLS = 2 * P
 RUN = 4
+LAG = 4
+VECTOR_HEAD = 640
+
+
+def gains_on_vector(tile):
+    return tile >= 36 and tile % 2 == 0 or tile == TILES - 1
+
+
+def evacuates_on_vector(tile):
+    return tile % 4 == 1 and tile < TILES // 2 or tile == TILES - 1
+
+
+def expanded_halves(n):
+    if n == 25:
+        return (19, 20)
+    if n == 26:
+        return (21, 22)
+    if n == 27:
+        return (23,)
+    return (n - 6,) if 6 <= n <= 24 else ()
 
 
 def tile_loreftsubspaceintervention_t_kernel(tc, h_bytes, h_scale, rot_in, w, b, g, rot_out, pw, out):
@@ -33,19 +56,20 @@ def tile_loreftsubspaceintervention_t_kernel(tc, h_bytes, h_scale, rot_in, w, b,
 
     with ExitStack() as ctx:
         keep = ctx.enter_context(tc.tile_pool(name="keep", bufs=1))
-        hb_pool = ctx.enter_context(tc.tile_pool(name="hb", bufs=3))
-        hg_pool = ctx.enter_context(tc.tile_pool(name="hg", bufs=4))
-        src_pool = ctx.enter_context(tc.tile_pool(name="src", bufs=3))
-        diff_pool = ctx.enter_context(tc.tile_pool(name="diff", bufs=8))
-        hq_pool = ctx.enter_context(tc.tile_pool(name="hq", bufs=5))
-        o_pool = ctx.enter_context(tc.tile_pool(name="o", bufs=4))
-        xt_psum = ctx.enter_context(tc.psum_pool(name="xt", bufs=2))
+        wide_pool = ctx.enter_context(tc.tile_pool(name="wide", bufs=4))
+        joint_pool = ctx.enter_context(tc.tile_pool(name="joint", bufs=6))
+        quant_pool = ctx.enter_context(tc.tile_pool(name="quant", bufs=5))
+        source_pool = ctx.enter_context(tc.tile_pool(name="source", bufs=3))
+        delta_pool = ctx.enter_context(tc.tile_pool(name="delta", bufs=8))
+        result_pool = ctx.enter_context(tc.tile_pool(name="result", bufs=4))
+        turn_psum = ctx.enter_context(tc.psum_pool(name="turn", bufs=2))
         pre_psum = ctx.enter_context(tc.psum_pool(name="pre", bufs=2))
         base_psum = ctx.enter_context(tc.psum_pool(name="base", bufs=2))
         edit_psum = ctx.enter_context(tc.psum_pool(name="edit", bufs=2))
 
         ident = keep.tile([P, P], F32)
-        h_raw = [keep.tile([P, 4, D], U8, name="h_raw_%d" % i) for i in range(GROUPS)]
+        warm = keep.tile([P, 1], F32)
+        h_codes_in = [keep.tile([P, TILES_PER_GROUP, D], U8, name="h_codes_in_%d" % i) for i in range(GROUPS)]
         k_scale = keep.tile([P, PACK], F32)
         rot_in_raw = keep.tile([P, 4, D], BF16)
         w_raw = keep.tile([P, PACK, R], BF16)
@@ -55,228 +79,266 @@ def tile_loreftsubspaceintervention_t_kernel(tc, h_bytes, h_scale, rot_in, w, b,
         gain_rows = keep.tile([P, P, PACK], F32)
         pw_raw = keep.tile([P, TILES], BF16)
         strength = keep.tile([P, TILES], F32)
-        warm = keep.tile([P, 1], F32)
-
         w_grouped = keep.tile([P, R * PACK], BF16, align_bytes=64)
         rot_in_grouped = keep.tile([P, R * PACK], BF16, align_bytes=64)
         rot_out_grouped = keep.tile([P, D * PACK], BF16, align_bytes=64)
-        w_q = (keep.tile([P, R], U32, align_bytes=64, name="w_codes"), keep.tile([P, R], U8, align_bytes=64, name="w_planes"))
-        rot_in_q = (keep.tile([P, R], U32, align_bytes=64, name="rot_in_codes"), keep.tile([P, R], U8, align_bytes=64, name="rot_in_planes"))
-        rot_out_q = (keep.tile([P, D], U32, align_bytes=64, name="rot_out_codes"), keep.tile([P, D], U8, align_bytes=64, name="rot_out_planes"))
+        w_q = (keep.tile([P, R], U32, align_bytes=64, name="w_codes"), keep.tile([P, R], U8, align_bytes=64, name="w_scales"))
+        rot_in_q = (
+            keep.tile([P, R], U32, align_bytes=64, name="rot_in_codes"),
+            keep.tile([P, R], U8, align_bytes=64, name="rot_in_scales"),
+        )
+        rot_out_q = (
+            keep.tile([P, D], U32, align_bytes=64, name="rot_out_codes"),
+            keep.tile([P, D], U8, align_bytes=64, name="rot_out_scales"),
+        )
+
+        wide, turned, joint, h_q, source, delta, diff_q, results = {}, {}, {}, {}, {}, {}, {}, {}
+        pres, bases, edits = [], [], []
+
+        def quantize(operand, cols, grouped):
+            codes, scales = operand
+            nc.vector.quantize_mx(out=codes[:, cols].bitcast(FP8X4), scales=scales[:, cols], in_=grouped)
+
+        def multiply(bank, left, left_cols, right, right_cols):
+            nc.tensor.matmul_mx(
+                out=bank,
+                lhsT=left[0][:, left_cols].bitcast(FP8X4),
+                lhsT_scale=left[1][:, left_cols],
+                rhs=right[0][:, right_cols].bitcast(FP8X4),
+                rhs_scale=right[1][:, right_cols],
+                start=True,
+                stop=True,
+            )
+
+
+        def widen(n):
+            group, half = divmod(n, 2)
+            codes = h_codes_in[group][:].rearrange("p j k -> p (j k)")[:, half * 2 * D : (half + 1) * 2 * D]
+            tokens = wide_pool.tile([P, 2 * D], BF16)
+            nc.scalar.copy(out=tokens[:], in_=codes.bitcast(FP8))
+            wide[n] = tokens
+
+        def widen_on_two_engines(n):
+            group, half = divmod(n, 2)
+            codes = h_codes_in[group][:].rearrange("p j k -> p (j k)")[:, half * 2 * D : (half + 1) * 2 * D]
+            tokens = wide_pool.tile([P, 2 * D], BF16)
+            nc.vector.tensor_copy(out=tokens[:, :VECTOR_HEAD], in_=codes[:, :VECTOR_HEAD].bitcast(FP8))
+            nc.scalar.copy(out=tokens[:, VECTOR_HEAD:], in_=codes[:, VECTOR_HEAD:].bitcast(FP8))
+            wide[n] = tokens
+
+        def turn(n):
+            bank = turn_psum.tile([P, 2, HALF_COLS], F32)
+            words = wide.pop(n)[:].bitcast(F32)
+            for j in range(2):
+                for u in range(2):
+                    nc.tensor.transpose(
+                        bank[:, u, j * P : (j + 1) * P],
+                        words[:, j * D // 2 + u : (j + 1) * D // 2 : 2],
+                        ident[:],
+                    )
+            turned[n] = bank
+
+        def joint_tile(i):
+            if i not in joint:
+                both = joint_pool.tile([P, 2 * COLS, PACK], BF16, align_bytes=64)
+                joint[i] = both
+            return joint[i]
+
+        def scale_h(n):
+            group, half = divmod(n, 2)
+            grouped = joint_tile(group)[:, half * HALF_COLS : (half + 1) * HALF_COLS, :]
+            pairs = turned.pop(n)[:].rearrange("p u c -> p (u c)").bitcast(BF16)
+            factor = k_scale[:].unsqueeze(1).to_broadcast([P, HALF_COLS, PACK])
+            nc.vector.tensor_tensor(
+                out=grouped.rearrange("p c (u e) -> p c u e", e=2),
+                in0=factor.rearrange("p c (u e) -> p c u e", e=2),
+                in1=pairs.rearrange("p (u c e) -> p c u e", u=2, e=2),
+                op=MULT,
+            )
+
+        def quantize_joint(i):
+            first = 0 if i < GROUPS else COLS
+            last = 2 * COLS if i >= LAG else COLS
+            parts = 2 if i == GROUPS + LAG - 1 else 1
+            width = (last - first) // parts
+            codes = quant_pool.tile([P, 2 * COLS], U32, align_bytes=64)
+            scales = quant_pool.tile([P, 2 * COLS], U8, align_bytes=64)
+            grouped = joint.pop(i)
+            for lo in range(first, last, width):
+                cols = slice(lo, lo + width)
+                quantize((codes, scales), cols, grouped[:, cols, :].rearrange("p c t -> p (c t)"))
+            if i < GROUPS:
+                h_q[i] = (codes[:, :COLS], scales[:, :COLS])
+            if i >= LAG:
+                diff_q[i - LAG] = (codes[:, COLS:], scales[:, COLS:])
+
+
+        def project_source(i, t):
+            if t == 0:
+                rows = source_pool.tile([P, PACK, COLS], F32)
+                source[i] = rows
+            pre = pre_psum.tile([P, COLS], F32)
+            multiply(pre[:], w_q, slice(t * P, (t + 1) * P), h_q[i], slice(0, COLS))
+            pres.append((i, t, pre))
+
+        def activate():
+            i, t, pre = pres.pop(0)
+            nc.scalar.activation(out=source[i][:, t, :], in_=pre[:], func=SILU, bias=bias[:, t : t + 1])
+
+        def project_base(i, j):
+            base = base_psum.tile([P, PACK, P], F32)
+            for t in range(PACK):
+                multiply(base[:, t, :], rot_in_q, slice(t * P, (t + 1) * P), h_q[i], slice(j * P, (j + 1) * P))
+            bases.append((i, j, base))
+
+        def subtract():
+            if bases:
+                i, j, base = bases.pop(0)
+                difference = delta_pool.tile([P, P, PACK], F32)
+                delta[TILES_PER_GROUP * i + j] = difference
+                nc.vector.tensor_tensor(
+                    out=difference[:].rearrange("p (c i) t -> p c t i", i=RUN),
+                    in0=source[i][:, :, j * P : (j + 1) * P].rearrange("p t (c i) -> p c t i", i=RUN),
+                    in1=base[:].rearrange("p t (c i) -> p c t i", i=RUN),
+                    op=SUBTRACT,
+                )
+
+        def apply_gain(n):
+            for tile in (2 * n, 2 * n + 1):
+                i, j = divmod(tile, TILES_PER_GROUP)
+                engine = nc.vector if gains_on_vector(tile) else nc.gpsimd
+                lo = COLS + j * P
+                engine.tensor_tensor(
+                    out=joint_tile(i + LAG)[:, lo : lo + P, :].rearrange("p c t -> p (c t)"),
+                    in0=delta.pop(tile)[:].rearrange("p c t -> p (c t)"),
+                    in1=gain_rows[:].rearrange("p c t -> p (c t)"),
+                    op=MULT,
+                )
+
+
+        def expand(i, j):
+            edit = edit_psum.tile([P, D], F32)
+            multiply(edit[:], diff_q[i], slice(j * P, (j + 1) * P), rot_out_q, slice(0, D))
+            edits.append((TILES_PER_GROUP * i + j, edit))
+
+        def finish():
+            tile, edit = edits.pop(0)
+            pair, side = divmod(tile, 2)
+            if side == 0:
+                rows = result_pool.tile([P, 2, D], F32)
+                results[pair] = rows
+            row = results[pair][:, side, :]
+            factor = strength[:, tile : tile + 1]
+            if evacuates_on_vector(tile):
+                nc.vector.tensor_scalar(out=row, in0=edit[:], scalar1=factor, scalar2=None, op0=MULT)
+            else:
+                nc.scalar.activation(out=row, in_=edit[:], func=COPY, scale=factor)
+            if side == 1:
+                nc.sync.dma_start(out=out_rows[:, tile - 1 : tile + 1, :], in_=results.pop(pair)[:])
+
+
+        def group_w():
+            dst = w_grouped[:].rearrange("p (t m j) -> p t m j", t=4, j=PACK)
+            src = w_raw[:].rearrange("p j (m t) -> p t m j", t=4)
+            nc.gpsimd.tensor_scalar(out=dst[:, 0:2], in0=src[:, 0:2], scalar1=1.0, scalar2=0.0, op0=MULT, op1=ADD)
+            nc.vector.tensor_copy(out=dst[:, 2:4], in_=src[:, 2:4])
+
+        def group_rot_in():
+            for t0 in (0, 2):
+                bank = edit_psum.tile([P, 2, HALF_COLS], F32, name="edit")
+                for s in range(2):
+                    words = rot_in_raw[:, t0 + s, :].bitcast(F32)
+                    for u in range(2):
+                        nc.tensor.transpose(bank[:, u, s * P : (s + 1) * P], words[:, u::2], ident[:])
+                dst = rot_in_grouped[:, t0 * P * PACK : (t0 + 2) * P * PACK].bitcast(F32)
+                nc.scalar.copy(out=dst.rearrange("p (c u) -> p c u", u=2), in_=bank[:].rearrange("p u c -> p c u"))
+
+        def group_rot_out():
+            dst = rot_out_grouped[:].rearrange("p (n j) -> p n j", j=PACK)
+            src = rot_out_raw[:].rearrange("p j n -> p n j")
+            for lo in range(0, D, P):
+                cols = slice(lo, lo + P)
+                nc.gpsimd.tensor_scalar(out=dst[:, cols, :], in0=src[:, cols, :], scalar1=1.0, scalar2=0.0, op0=MULT, op1=ADD)
+
+        def step(n):
+            if n % 2 == 1 and n < HALVES:
+                quantize_joint((n + 3) // 2)
+            if pres:
+                activate()
+            if edits:
+                finish()
+            while pres:
+                activate()
+            for k in range(2):
+                if n % 2 == 0 and n + 4 + k < HALVES:
+                    scale_h(n + 4 + k)
+                subtract()
+            if edits:
+                finish()
+            if 0 <= n - 2 < HALVES:
+                apply_gain(n - 2)
+            if n == HALVES:
+                quantize_joint(GROUPS + LAG - 2)
+            if n == HALVES + 2:
+                quantize_joint(GROUPS + LAG - 1)
+            if n + 7 < HALVES:
+                widen(n + 7)
+            for k in range(2):
+                if 0 < n + 1 < HALVES:
+                    project_source((n + 1) // 2, 2 * ((n + 1) % 2) + k)
+                for m in expanded_halves(n):
+                    if len(edits) == 2:
+                        finish()
+                    expand(m // 2, 2 * (m % 2) + k)
+                if k == 1 and n + 6 < HALVES:
+                    turn(n + 6)
+                if 0 <= n - 1 < HALVES:
+                    project_base((n - 1) // 2, 2 * ((n - 1) % 2) + k)
 
         with tc.manual_schedule():
-            nc.sync.dma_start(out=h_raw[0][:], in_=h_rows[:, 0:4, :])
+            nc.sync.dma_start(out=h_codes_in[0][:], in_=h_rows[:, 0:4, :])
             nc.sync.dma_start(out=k_scale[:], in_=h_scale.rearrange("o (p t) -> p (o t)", t=PACK))
+            nc.sync.dma_start(out=h_codes_in[1][:], in_=h_rows[:, 4:8, :])
             nc.sync.dma_start(out=w_raw[:], in_=w.rearrange("(p j) c -> p j c", j=PACK))
-            nc.sync.dma_start(out=h_raw[1][:], in_=h_rows[:, 4:8, :])
             nc.sync.dma_start(out=rot_in_raw[:], in_=rot_in.rearrange("(m t) k -> m t k", t=4))
             nc.sync.dma_start(out=bias[:], in_=b.rearrange("(p t) -> p t", t=PACK))
+            nc.sync.dma_start(out=h_codes_in[2][:], in_=h_rows[:, 8:12, :])
             nc.sync.dma_start(out=gain[:], in_=g.rearrange("(p t) -> p t", t=PACK))
             nc.sync.dma_start(out=rot_out_raw[:], in_=rot_out.rearrange("(p j) n -> p j n", j=PACK))
             nc.sync.dma_start(out=pw_raw[:], in_=pw.rearrange("(p i) -> p i", p=P))
-            for i in range(2, GROUPS):
-                nc.sync.dma_start(out=h_raw[i][:], in_=h_rows[:, 4 * i : 4 * i + 4, :])
+            for i in range(3, GROUPS):
+                nc.sync.dma_start(out=h_codes_in[i][:], in_=h_rows[:, 4 * i : 4 * i + 4, :])
 
             nc.vector.memset(warm[:], 0.0)
-            nc.scalar.activation(out=warm[:], in_=warm[:], func=ACT.Silu)
+            nc.scalar.activation(out=warm[:], in_=warm[:], func=SILU)
             make_identity(nc, ident[:])
 
-            pres, bases, edits, results = [], [], [], {}
-            hb, xt, joint, hq, src, diff, dq = {}, {}, {}, {}, {}, {}, {}
-
-            def widen(n, copy):
-                i, half = divmod(n, 2)
-                codes = h_raw[i][:].rearrange("p j k -> p (j k)")
-                tokens = hb_pool.tile([P, 2 * D], BF16)
-                lo = half * 2 * D
-                copy(out=tokens[:], in_=codes[:, lo : lo + 2 * D].bitcast(FP8))
-                hb[n] = tokens
-
-            def turn(n):
-                bank = xt_psum.tile([P, 2, HCOLS], F32)
-                words = hb.pop(n)[:].bitcast(F32)
-                for j in range(2):
-                    for u in range(2):
-                        nc.tensor.transpose(bank[:, u, j * P : (j + 1) * P], words[:, j * 256 + u : (j + 1) * 256 : 2], ident[:])
-                xt[n] = bank
-
-            def get_joint(i):
-                if i not in joint:
-                    both = hg_pool.tile([P, 2 * COLS, PACK], BF16, align_bytes=64)
-                    joint[i] = both
-                return joint[i]
-
-            def scale_h(n):
-                i, half = divmod(n, 2)
-                if half == 0:
-                    get_joint(i)
-                dst = joint[i][:, half * HCOLS : (half + 1) * HCOLS, :].rearrange("p c (u e) -> p c u e", e=2)
-                words = xt.pop(n)[:].rearrange("p u c -> p (u c)").bitcast(BF16).rearrange("p (u c e) -> p c u e", u=2, e=2)
-                fac = k_scale[:].unsqueeze(1).to_broadcast([P, HCOLS, PACK]).rearrange("p c (u e) -> p c u e", e=2)
-                nc.vector.tensor_tensor(out=dst, in0=fac, in1=words, op=ALU.mult)
-
-            def quantize(codes, planes, grouped):
-                nc.vector.quantize_mx(out=codes.bitcast(FP8X4), scales=planes, in_=grouped)
-
-            def quantize_joint(i):
-                first = 0 if i < GROUPS else COLS
-                last = 2 * COLS if i >= LAG else COLS
-                parts = 2 if i == GROUPS + LAG - 1 else 1
-                width = (last - first) // parts
-                codes = hq_pool.tile([P, 2 * COLS], U32, align_bytes=64)
-                planes = hq_pool.tile([P, 2 * COLS], U8, align_bytes=64)
-                grouped = joint.pop(i)
-                for lo in range(first, last, width):
-                    cols = slice(lo, lo + width)
-                    quantize(codes[:, cols], planes[:, cols], grouped[:, cols, :].rearrange("p c t -> p (c t)"))
-                if i < GROUPS:
-                    hq[i] = (codes[:, :COLS], planes[:, :COLS])
-                if i >= LAG:
-                    dq[i - LAG] = (codes[:, COLS:], planes[:, COLS:])
-
-            def multiply(bank, left, left_cols, right, right_cols):
-                nc.tensor.matmul_mx(
-                    out=bank,
-                    lhsT=left[0][:, left_cols].bitcast(FP8X4),
-                    lhsT_scale=left[1][:, left_cols],
-                    rhs=right[0][:, right_cols].bitcast(FP8X4),
-                    rhs_scale=right[1][:, right_cols],
-                    start=True,
-                    stop=True,
-                )
-
-            def project_source(i, t):
-                if t == 0:
-                    source = src_pool.tile([P, 4, COLS], F32)
-                    src[i] = source
-                pre = pre_psum.tile([P, COLS], F32)
-                multiply(pre[:], w_q, slice(t * P, (t + 1) * P), hq[i], slice(0, COLS))
-                pres.append((i, t, pre))
-
-            def activate():
-                i, t, pre = pres.pop(0)
-                nc.scalar.activation(out=src[i][:, t, :], in_=pre[:], func=ACT.Silu, bias=bias[:, t : t + 1])
-
-            def project_base(i, j):
-                base = base_psum.tile([P, 4, P], F32)
-                for t in range(4):
-                    multiply(base[:, t, :], rot_in_q, slice(t * P, (t + 1) * P), hq[i], slice(j * P, (j + 1) * P))
-                bases.append((i, j, base))
-
-            def subtract():
-                while bases:
-                    i, j, base = bases.pop(0)
-                    cols = slice(j * P, (j + 1) * P)
-                    delta = diff_pool.tile([P, P, PACK], F32)
-                    diff[4 * i + j] = delta
-                    nc.vector.tensor_tensor(
-                        out=delta[:].rearrange("p (c i) t -> p c t i", i=RUN),
-                        in0=src[i][:, :, cols].rearrange("p t (c i) -> p c t i", i=RUN),
-                        in1=base[:].rearrange("p t (c i) -> p c t i", i=RUN),
-                        op=ALU.subtract,
-                    )
-
-            def apply_gain(n):
-                for tile in (2 * n, 2 * n + 1):
-                    i, j = divmod(tile, 4)
-                    engine = nc.vector if tile >= TILES - 2 else nc.gpsimd
-                    lo = COLS + j * P
-                    engine.tensor_tensor(
-                        out=get_joint(i + LAG)[:, lo : lo + P, :].rearrange("p c t -> p (c t)"),
-                        in0=diff.pop(tile)[:].rearrange("p c t -> p (c t)"),
-                        in1=gain_rows[:].rearrange("p c t -> p (c t)"),
-                        op=ALU.mult,
-                    )
-
-            def expand(i, j):
-                edit = edit_psum.tile([P, D], F32)
-                multiply(edit[:], dq[i], slice(j * P, (j + 1) * P), rot_out_q, slice(0, D))
-                edits.append((4 * i + j, edit))
-
-            def finish():
-                tile, edit = edits.pop(0)
-                if tile % 2 == 0:
-                    rows = o_pool.tile([P, 2, D], F32)
-                    results[tile // 2] = rows
-                row = results[tile // 2][:, tile % 2, :]
-                if tile % 6 == 5:
-                    nc.vector.tensor_scalar(out=row, in0=edit[:], scalar1=strength[:, tile : tile + 1], scalar2=None, op0=ALU.mult)
-                else:
-                    nc.scalar.activation(out=row, in_=edit[:], func=ACT.Copy, scale=strength[:, tile : tile + 1])
-                if tile % 2 == 1:
-                    nc.sync.dma_start(out=out_rows[:, tile - 1 : tile + 1, :], in_=results.pop(tile // 2)[:])
-
-            def w_interleave():
-                dst = w_grouped[:].rearrange("p (t m j) -> p t m j", t=4, j=PACK)
-                src = w_raw[:].rearrange("p j (m t) -> p t m j", t=4)
-                nc.gpsimd.tensor_scalar(out=dst[:, 0:2], in0=src[:, 0:2], scalar1=1.0, scalar2=0.0, op0=ALU.mult, op1=ALU.add)
-                nc.vector.tensor_copy(out=dst[:, 2:4], in_=src[:, 2:4])
-
-            def rot_in_turn():
-                for t0 in (0, 2):
-                    bank = edit_psum.tile([P, 2, HCOLS], F32, name="edit")
-                    for s in range(2):
-                        words = rot_in_raw[:, t0 + s, :].bitcast(F32)
-                        for u in range(2):
-                            nc.tensor.transpose(bank[:, u, s * P : (s + 1) * P], words[:, u::2], ident[:])
-                    dst = rot_in_grouped[:, t0 * COLS : (t0 + 2) * COLS].bitcast(F32).rearrange("p (c u) -> p c u", u=2)
-                    nc.scalar.copy(out=dst, in_=bank[:].rearrange("p u c -> p c u"))
-
-            def multiplies(n, k):
-                if 0 <= n - 2 < HALVES:
-                    project_base((n - 2) // 2, 2 * (n % 2) + k)
-                if 0 <= n < HALVES:
-                    project_source(n // 2, 2 * (n % 2) + k)
-                if 0 <= n - 6 < HALVES:
-                    expand((n - 6) // 2, 2 * (n % 2) + k)
-
-            def step(n):
-                subtract()
-                for k in range(2):
-                    if pres:
-                        activate()
-                    if edits:
-                        finish()
-                if 0 <= n - 3 < HALVES:
-                    apply_gain(n - 3)
-                if n % 2 == 1 and 0 <= (n + 1) // 2 < GROUPS + LAG:
-                    quantize_joint((n + 1) // 2)
-                if 0 <= n + 3 < HALVES:
-                    scale_h(n + 3)
-                if 0 <= n + 5 < HALVES:
-                    widen(n + 5, nc.scalar.copy)
-                multiplies(n, 0)
-                if 0 <= n + 4 < HALVES:
-                    turn(n + 4)
-                multiplies(n, 1)
-
-            widen(0, nc.scalar.copy)
-            widen(1, nc.vector.tensor_copy)
+            widen_on_two_engines(0)
+            widen_on_two_engines(1)
             turn(0)
-            w_interleave()
             turn(1)
+            widen(2)
             scale_h(0)
             scale_h(1)
-            quantize(w_q[0][:], w_q[1][:], w_grouped[:])
-            quantize_joint(0)
-            widen(2, nc.scalar.copy)
-            widen(3, nc.scalar.copy)
+            group_w()
             turn(2)
+            widen(3)
+            group_rot_in()
+            quantize(w_q, slice(0, R), w_grouped[:])
+            quantize_joint(0)
+            project_source(0, 0)
+            project_source(0, 1)
             turn(3)
-            rot_in_turn()
-            scale_h(2)
-            widen(4, nc.scalar.copy)
-            step(0)
-            quantize(rot_in_q[0][:], rot_in_q[1][:], rot_in_grouped[:])
-            nc.vector.tensor_copy(out=gain_rows[:], in_=gain[:].unsqueeze(1).to_broadcast([P, P, PACK]))
-            nc.vector.tensor_copy(out=strength[:], in_=pw_raw[:])
-            nc.gpsimd.tensor_scalar(
-                out=rot_out_grouped[:].rearrange("p (n j) -> p n j", j=PACK),
-                in0=rot_out_raw[:].rearrange("p j n -> p n j"),
-                scalar1=1.0, scalar2=0.0, op0=ALU.mult, op1=ALU.add,
-            )
-            step(1)
-            step(2)
-            quantize(rot_out_q[0][:], rot_out_q[1][:], rot_out_grouped[:])
-            for n in range(3, HALVES + 7):
+            widen(4)
+            activate()
+            activate()
+            nc.scalar.copy(out=gain_rows[:], in_=gain[:].unsqueeze(1).to_broadcast([P, P, PACK]))
+            nc.scalar.copy(out=strength[:], in_=pw_raw[:])
+            group_rot_out()
+            step(-2)
+            quantize(rot_in_q, slice(0, R), rot_in_grouped[:])
+            for n in range(-1, 3):
+                step(n)
+            quantize(rot_out_q, slice(0, D), rot_out_grouped[:])
+            for n in range(3, HALVES + 5):
                 step(n)

from contextlib import ExitStack

import concourse.mybir as mybir
from concourse.masks import make_identity

T, D, R = 6144, 512, 512
FLOPS = 3 * 2 * T * D * R

F32 = mybir.dt.float32
BF16 = mybir.dt.bfloat16
U32 = mybir.dt.uint32
U8 = mybir.dt.uint8
FP8 = mybir.dt.float8_e4m3fn
FP8X4 = mybir.dt.float8_e4m3fn_x4
MULT = mybir.AluOpType.mult
ADD = mybir.AluOpType.add
SUBTRACT = mybir.AluOpType.subtract
COPY = mybir.ActivationFunctionType.Copy
SILU = mybir.ActivationFunctionType.Silu

P = 128
PACK = 4
TILES = T // P
TILES_PER_GROUP = 4
GROUPS = TILES // TILES_PER_GROUP
HALVES = 2 * GROUPS
COLS = TILES_PER_GROUP * P
HALF_COLS = 2 * P
RUN = 4
LAG = 4
VECTOR_HEAD = 640


def gains_on_vector(tile):
    return tile >= 36 and tile % 2 == 0 or tile == TILES - 1


def evacuates_on_vector(tile):
    return tile % 4 == 1 and tile < TILES // 2 or tile == TILES - 1


def expanded_halves(n):
    if n == 25:
        return (19, 20)
    if n == 26:
        return (21, 22)
    if n == 27:
        return (23,)
    return (n - 6,) if 6 <= n <= 24 else ()


def tile_loreftsubspaceintervention_t_kernel(tc, h_bytes, h_scale, rot_in, w, b, g, rot_out, pw, out):
    nc = tc.nc
    h_rows = h_bytes.rearrange("(p i) k -> p i k", p=P)
    out_rows = out.rearrange("(p i) d -> p i d", p=P)

    with ExitStack() as ctx:
        keep = ctx.enter_context(tc.tile_pool(name="keep", bufs=1))
        wide_pool = ctx.enter_context(tc.tile_pool(name="wide", bufs=4))
        joint_pool = ctx.enter_context(tc.tile_pool(name="joint", bufs=6))
        quant_pool = ctx.enter_context(tc.tile_pool(name="quant", bufs=5))
        source_pool = ctx.enter_context(tc.tile_pool(name="source", bufs=3))
        delta_pool = ctx.enter_context(tc.tile_pool(name="delta", bufs=8))
        result_pool = ctx.enter_context(tc.tile_pool(name="result", bufs=4))
        turn_psum = ctx.enter_context(tc.psum_pool(name="turn", bufs=2))
        pre_psum = ctx.enter_context(tc.psum_pool(name="pre", bufs=2))
        base_psum = ctx.enter_context(tc.psum_pool(name="base", bufs=2))
        edit_psum = ctx.enter_context(tc.psum_pool(name="edit", bufs=2))

        ident = keep.tile([P, P], F32)
        warm = keep.tile([P, 1], F32)
        h_codes_in = [keep.tile([P, TILES_PER_GROUP, D], U8, name="h_codes_in_%d" % i) for i in range(GROUPS)]
        k_scale = keep.tile([P, PACK], F32)
        rot_in_raw = keep.tile([P, 4, D], BF16)
        w_raw = keep.tile([P, PACK, R], BF16)
        rot_out_raw = keep.tile([P, PACK, D], BF16)
        bias = keep.tile([P, PACK], BF16)
        gain = keep.tile([P, PACK], BF16)
        gain_rows = keep.tile([P, P, PACK], F32)
        pw_raw = keep.tile([P, TILES], BF16)
        strength = keep.tile([P, TILES], F32)
        w_grouped = keep.tile([P, R * PACK], BF16, align_bytes=64)
        rot_in_grouped = keep.tile([P, R * PACK], BF16, align_bytes=64)
        rot_out_grouped = keep.tile([P, D * PACK], BF16, align_bytes=64)
        w_q = (keep.tile([P, R], U32, align_bytes=64, name="w_codes"), keep.tile([P, R], U8, align_bytes=64, name="w_scales"))
        rot_in_q = (
            keep.tile([P, R], U32, align_bytes=64, name="rot_in_codes"),
            keep.tile([P, R], U8, align_bytes=64, name="rot_in_scales"),
        )
        rot_out_q = (
            keep.tile([P, D], U32, align_bytes=64, name="rot_out_codes"),
            keep.tile([P, D], U8, align_bytes=64, name="rot_out_scales"),
        )

        wide, turned, joint, h_q, source, delta, diff_q, results = {}, {}, {}, {}, {}, {}, {}, {}
        pres, bases, edits = [], [], []

        def quantize(operand, cols, grouped):
            codes, scales = operand
            nc.vector.quantize_mx(out=codes[:, cols].bitcast(FP8X4), scales=scales[:, cols], in_=grouped)

        def multiply(bank, left, left_cols, right, right_cols):
            nc.tensor.matmul_mx(
                out=bank,
                lhsT=left[0][:, left_cols].bitcast(FP8X4),
                lhsT_scale=left[1][:, left_cols],
                rhs=right[0][:, right_cols].bitcast(FP8X4),
                rhs_scale=right[1][:, right_cols],
                start=True,
                stop=True,
            )


        def widen(n):
            group, half = divmod(n, 2)
            codes = h_codes_in[group][:].rearrange("p j k -> p (j k)")[:, half * 2 * D : (half + 1) * 2 * D]
            tokens = wide_pool.tile([P, 2 * D], BF16)
            nc.scalar.copy(out=tokens[:], in_=codes.bitcast(FP8))
            wide[n] = tokens

        def widen_on_two_engines(n):
            group, half = divmod(n, 2)
            codes = h_codes_in[group][:].rearrange("p j k -> p (j k)")[:, half * 2 * D : (half + 1) * 2 * D]
            tokens = wide_pool.tile([P, 2 * D], BF16)
            nc.vector.tensor_copy(out=tokens[:, :VECTOR_HEAD], in_=codes[:, :VECTOR_HEAD].bitcast(FP8))
            nc.scalar.copy(out=tokens[:, VECTOR_HEAD:], in_=codes[:, VECTOR_HEAD:].bitcast(FP8))
            wide[n] = tokens

        def turn(n):
            bank = turn_psum.tile([P, 2, HALF_COLS], F32)
            words = wide.pop(n)[:].bitcast(F32)
            for j in range(2):
                for u in range(2):
                    nc.tensor.transpose(
                        bank[:, u, j * P : (j + 1) * P],
                        words[:, j * D // 2 + u : (j + 1) * D // 2 : 2],
                        ident[:],
                    )
            turned[n] = bank

        def joint_tile(i):
            if i not in joint:
                both = joint_pool.tile([P, 2 * COLS, PACK], BF16, align_bytes=64)
                joint[i] = both
            return joint[i]

        def scale_h(n):
            group, half = divmod(n, 2)
            grouped = joint_tile(group)[:, half * HALF_COLS : (half + 1) * HALF_COLS, :]
            pairs = turned.pop(n)[:].rearrange("p u c -> p (u c)").bitcast(BF16)
            factor = k_scale[:].unsqueeze(1).to_broadcast([P, HALF_COLS, PACK])
            nc.vector.tensor_tensor(
                out=grouped.rearrange("p c (u e) -> p c u e", e=2),
                in0=factor.rearrange("p c (u e) -> p c u e", e=2),
                in1=pairs.rearrange("p (u c e) -> p c u e", u=2, e=2),
                op=MULT,
            )

        def quantize_joint(i):
            first = 0 if i < GROUPS else COLS
            last = 2 * COLS if i >= LAG else COLS
            parts = 2 if i == GROUPS + LAG - 1 else 1
            width = (last - first) // parts
            codes = quant_pool.tile([P, 2 * COLS], U32, align_bytes=64)
            scales = quant_pool.tile([P, 2 * COLS], U8, align_bytes=64)
            grouped = joint.pop(i)
            for lo in range(first, last, width):
                cols = slice(lo, lo + width)
                quantize((codes, scales), cols, grouped[:, cols, :].rearrange("p c t -> p (c t)"))
            if i < GROUPS:
                h_q[i] = (codes[:, :COLS], scales[:, :COLS])
            if i >= LAG:
                diff_q[i - LAG] = (codes[:, COLS:], scales[:, COLS:])


        def project_source(i, t):
            if t == 0:
                rows = source_pool.tile([P, PACK, COLS], F32)
                source[i] = rows
            pre = pre_psum.tile([P, COLS], F32)
            multiply(pre[:], w_q, slice(t * P, (t + 1) * P), h_q[i], slice(0, COLS))
            pres.append((i, t, pre))

        def activate():
            i, t, pre = pres.pop(0)
            nc.scalar.activation(out=source[i][:, t, :], in_=pre[:], func=SILU, bias=bias[:, t : t + 1])

        def project_base(i, j):
            base = base_psum.tile([P, PACK, P], F32)
            for t in range(PACK):
                multiply(base[:, t, :], rot_in_q, slice(t * P, (t + 1) * P), h_q[i], slice(j * P, (j + 1) * P))
            bases.append((i, j, base))

        def subtract():
            if bases:
                i, j, base = bases.pop(0)
                difference = delta_pool.tile([P, P, PACK], F32)
                delta[TILES_PER_GROUP * i + j] = difference
                nc.vector.tensor_tensor(
                    out=difference[:].rearrange("p (c i) t -> p c t i", i=RUN),
                    in0=source[i][:, :, j * P : (j + 1) * P].rearrange("p t (c i) -> p c t i", i=RUN),
                    in1=base[:].rearrange("p t (c i) -> p c t i", i=RUN),
                    op=SUBTRACT,
                )

        def apply_gain(n):
            for tile in (2 * n, 2 * n + 1):
                i, j = divmod(tile, TILES_PER_GROUP)
                engine = nc.vector if gains_on_vector(tile) else nc.gpsimd
                lo = COLS + j * P
                engine.tensor_tensor(
                    out=joint_tile(i + LAG)[:, lo : lo + P, :].rearrange("p c t -> p (c t)"),
                    in0=delta.pop(tile)[:].rearrange("p c t -> p (c t)"),
                    in1=gain_rows[:].rearrange("p c t -> p (c t)"),
                    op=MULT,
                )


        def expand(i, j):
            edit = edit_psum.tile([P, D], F32)
            multiply(edit[:], diff_q[i], slice(j * P, (j + 1) * P), rot_out_q, slice(0, D))
            edits.append((TILES_PER_GROUP * i + j, edit))

        def finish():
            tile, edit = edits.pop(0)
            pair, side = divmod(tile, 2)
            if side == 0:
                rows = result_pool.tile([P, 2, D], F32)
                results[pair] = rows
            row = results[pair][:, side, :]
            factor = strength[:, tile : tile + 1]
            if evacuates_on_vector(tile):
                nc.vector.tensor_scalar(out=row, in0=edit[:], scalar1=factor, scalar2=None, op0=MULT)
            else:
                nc.scalar.activation(out=row, in_=edit[:], func=COPY, scale=factor)
            if side == 1:
                nc.sync.dma_start(out=out_rows[:, tile - 1 : tile + 1, :], in_=results.pop(pair)[:])


        def group_w():
            dst = w_grouped[:].rearrange("p (t m j) -> p t m j", t=4, j=PACK)
            src = w_raw[:].rearrange("p j (m t) -> p t m j", t=4)
            nc.gpsimd.tensor_scalar(out=dst[:, 0:2], in0=src[:, 0:2], scalar1=1.0, scalar2=0.0, op0=MULT, op1=ADD)
            nc.vector.tensor_copy(out=dst[:, 2:4], in_=src[:, 2:4])

        def group_rot_in():
            for t0 in (0, 2):
                bank = edit_psum.tile([P, 2, HALF_COLS], F32, name="edit")
                for s in range(2):
                    words = rot_in_raw[:, t0 + s, :].bitcast(F32)
                    for u in range(2):
                        nc.tensor.transpose(bank[:, u, s * P : (s + 1) * P], words[:, u::2], ident[:])
                dst = rot_in_grouped[:, t0 * P * PACK : (t0 + 2) * P * PACK].bitcast(F32)
                nc.scalar.copy(out=dst.rearrange("p (c u) -> p c u", u=2), in_=bank[:].rearrange("p u c -> p c u"))

        def group_rot_out():
            dst = rot_out_grouped[:].rearrange("p (n j) -> p n j", j=PACK)
            src = rot_out_raw[:].rearrange("p j n -> p n j")
            for lo in range(0, D, P):
                cols = slice(lo, lo + P)
                nc.gpsimd.tensor_scalar(out=dst[:, cols, :], in0=src[:, cols, :], scalar1=1.0, scalar2=0.0, op0=MULT, op1=ADD)

        def step(n):
            if n % 2 == 1 and n < HALVES:
                quantize_joint((n + 3) // 2)
            if pres:
                activate()
            if edits:
                finish()
            while pres:
                activate()
            for k in range(2):
                if n % 2 == 0 and n + 4 + k < HALVES:
                    scale_h(n + 4 + k)
                subtract()
            if edits:
                finish()
            if 0 <= n - 2 < HALVES:
                apply_gain(n - 2)
            if n == HALVES:
                quantize_joint(GROUPS + LAG - 2)
            if n == HALVES + 2:
                quantize_joint(GROUPS + LAG - 1)
            if n + 7 < HALVES:
                widen(n + 7)
            for k in range(2):
                if 0 < n + 1 < HALVES:
                    project_source((n + 1) // 2, 2 * ((n + 1) % 2) + k)
                for m in expanded_halves(n):
                    if len(edits) == 2:
                        finish()
                    expand(m // 2, 2 * (m % 2) + k)
                if k == 1 and n + 6 < HALVES:
                    turn(n + 6)
                if 0 <= n - 1 < HALVES:
                    project_base((n - 1) // 2, 2 * ((n - 1) % 2) + k)

        with tc.manual_schedule():
            nc.sync.dma_start(out=h_codes_in[0][:], in_=h_rows[:, 0:4, :])
            nc.sync.dma_start(out=k_scale[:], in_=h_scale.rearrange("o (p t) -> p (o t)", t=PACK))
            nc.sync.dma_start(out=h_codes_in[1][:], in_=h_rows[:, 4:8, :])
            nc.sync.dma_start(out=w_raw[:], in_=w.rearrange("(p j) c -> p j c", j=PACK))
            nc.sync.dma_start(out=rot_in_raw[:], in_=rot_in.rearrange("(m t) k -> m t k", t=4))
            nc.sync.dma_start(out=bias[:], in_=b.rearrange("(p t) -> p t", t=PACK))
            nc.sync.dma_start(out=h_codes_in[2][:], in_=h_rows[:, 8:12, :])
            nc.sync.dma_start(out=gain[:], in_=g.rearrange("(p t) -> p t", t=PACK))
            nc.sync.dma_start(out=rot_out_raw[:], in_=rot_out.rearrange("(p j) n -> p j n", j=PACK))
            nc.sync.dma_start(out=pw_raw[:], in_=pw.rearrange("(p i) -> p i", p=P))
            for i in range(3, GROUPS):
                nc.sync.dma_start(out=h_codes_in[i][:], in_=h_rows[:, 4 * i : 4 * i + 4, :])

            nc.vector.memset(warm[:], 0.0)
            nc.scalar.activation(out=warm[:], in_=warm[:], func=SILU)
            make_identity(nc, ident[:])

            widen_on_two_engines(0)
            widen_on_two_engines(1)
            turn(0)
            turn(1)
            widen(2)
            scale_h(0)
            scale_h(1)
            group_w()
            turn(2)
            widen(3)
            group_rot_in()
            quantize(w_q, slice(0, R), w_grouped[:])
            quantize_joint(0)
            project_source(0, 0)
            project_source(0, 1)
            turn(3)
            widen(4)
            activate()
            activate()
            nc.scalar.copy(out=gain_rows[:], in_=gain[:].unsqueeze(1).to_broadcast([P, P, PACK]))
            nc.scalar.copy(out=strength[:], in_=pw_raw[:])
            group_rot_out()
            step(-2)
            quantize(rot_in_q, slice(0, R), rot_in_grouped[:])
            for n in range(-1, 3):
                step(n)
            quantize(rot_out_q, slice(0, D), rot_out_grouped[:])
            for n in range(3, HALVES + 5):
                step(n)
